import numpy as np
import ml_dtypes


def mxq(x, axis, fmt="e4m3"):
    dtype, down = {"e4m3": (ml_dtypes.float8_e4m3fn, 7), "e5m2": (ml_dtypes.float8_e5m2, 14)}[fmt]
    v = np.moveaxis(np.asarray(x, np.float32).astype(ml_dtypes.bfloat16).astype(np.float64), axis, -1)
    blocks = v.reshape(v.shape[:-1] + (-1, 32))
    amax = np.abs(blocks).max(-1, keepdims=True)
    byte = np.maximum(np.where(amax > 0, np.frexp(amax)[1] - 1 + 127, 0) - down, 1)
    scale = np.exp2(byte - 127.0)
    codes = (blocks / scale).astype(np.float32).astype(dtype).astype(np.float64)
    return np.moveaxis((codes * scale).reshape(v.shape), -1, axis)


WIDE = False


def mx_kscale(k):
    if not WIDE:
        return np.ones(k)
    levels = np.array([10, -10, 5, -5, 0])
    if k % 512:
        return np.exp2(np.random.permutation(np.resize(levels, k // 32))).repeat(32)
    a = np.empty((k // 512, 16))
    for p in range(k // 512):
        a[p, :8] = np.random.permutation(np.resize(levels, 8))
        for g in range(8):
            far = levels[np.abs(levels - a[p, g]) >= 10]
            a[p, g + 8] = far[np.random.randint(len(far))]
    return np.exp2(a.ravel()).repeat(32)


def f64(x):
    return np.asarray(x).astype(np.float64)


def striped(idx):
    return np.tile(idx.reshape(-1, 16).T, (8, 1)).astype(np.uint16)


def unstriped(offs):
    return offs[:16].T.reshape(-1).astype(np.int64)


E2M1 = np.array([0.0, 0.5, 1.0, 1.5, 2.0, 3.0, 4.0, 6.0, -0.0, -0.5, -1.0, -1.5, -2.0, -3.0, -4.0, -6.0])


def pack_weight(w, fmt):
    k, n = w.shape
    w = f64(np.asarray(w, np.float32).astype(ml_dtypes.bfloat16)).reshape(k // 32, 32, n)
    amax = np.abs(w).max(1)
    if fmt == "e4m3":
        byte = np.frexp(amax)[1] - 1 + 127 - 7
    else:
        mant, ex = np.frexp(amax / 6.0)
        byte = np.where(mant > 0.5, ex, ex - 1) + 127
    byte = np.clip(np.where(amax > 0, byte, 1), 1, 254)
    scaled = (w * np.exp2(127.0 - byte)[:, None, :]).reshape(k, n).astype(np.float32)
    by_word = np.ascontiguousarray(scaled.reshape(k // 512, 128, 4, n).transpose(0, 1, 3, 2))
    if fmt == "e4m3":
        words = by_word.astype(ml_dtypes.float8_e4m3fn).view(np.uint8)
    else:
        c = by_word.astype(ml_dtypes.float4_e2m1fn).view(np.uint8) & 0xF
        words = (c[..., 0::2] | (c[..., 1::2] << 4)).reshape(k // 512, 128, 2 * n)
    return np.ascontiguousarray(words), np.ascontiguousarray(byte.astype(np.uint8).reshape(k // 512, 16, n))


def unpack_weight(words, scales, fmt):
    g, _, n = scales.shape
    words = np.ascontiguousarray(words).reshape(g, 128, n, -1)
    if fmt == "e4m3":
        vals = words.view(ml_dtypes.float8_e4m3fn).astype(np.float64)
    else:
        nib = np.empty((g, 128, n, 4), np.uint8)
        nib[..., 0::2] = words & 0xF
        nib[..., 1::2] = words >> 4
        vals = E2M1[nib]
    vals = vals * np.repeat(np.exp2(scales.astype(np.float64) - 127.0), 8, axis=1)[..., None]
    return vals.transpose(0, 1, 3, 2).reshape(g * 512, n)


def gelu(v):
    return 0.5 * v * (1.0 + np.tanh(np.sqrt(2.0 / np.pi) * (v + 0.044715 * v**3)))


def striped8(idx):
    return np.concatenate([v.reshape(-1, 16).T for v in idx]).astype(np.uint16)


def unstriped8(offs):
    return np.stack([offs[16 * g:16 * g + 16].T.reshape(-1) for g in range(8)]).astype(np.int64)


def heads(h, wgt, idx8):
    r = np.arange(h.shape[0])
    return wgt[r // 4 % 128] * h[r[:, None], idx8[r % 512 // 64]]


K, H, T, S, P = 1536, 512, 4096, 1024, 512


def setup_inputs():
    n = np.random.standard_normal
    s = mx_kscale(K)[:, None]
    u = mx_kscale(H)[:, None]
    tab_words, tab_scales = pack_weight(n((K, T)) * s, "e4m3")
    w1 = (n((K, H)) / s / np.sqrt(K)).astype(np.float32)
    gain = (0.2 * np.random.uniform(0.8, 1.2, H)).astype(np.float32)
    wga = np.repeat(np.random.uniform(0.5, 2.0, (8, P)), 16, axis=0).astype(np.float32)
    wgb = np.repeat(np.random.uniform(0.5, 2.0, (8, P)), 16, axis=0).astype(np.float32)
    amp = (1.5 * np.exp(0.3 * n(H)) * u[:, 0]).astype(np.float32)
    w2_words, w2_scales = pack_weight(2.0 * n((H, H)) / u / np.sqrt(H), "e2m1")
    offs = striped(np.random.permutation(T)[:S])
    offs2 = striped8(np.stack([np.random.permutation(S)[:P] for _ in range(8)]))
    offs3 = striped8(np.stack([np.random.permutation(S)[:P] for _ in range(8)]))
    return {"tab_words": tab_words, "tab_scales": tab_scales, "offs": offs, "w1": w1, "gain": gain,
            "offs2": offs2, "wga": wga, "offs3": offs3, "wgb": wgb, "amp": amp,
            "w2_words": w2_words, "w2_scales": w2_scales}


def reference(tab_words, tab_scales, offs, w1, gain, offs2, wga, offs3, wgb, amp, w2_words, w2_scales):
    v = unpack_weight(tab_words, tab_scales, "e4m3")[:, unstriped(offs)]
    h = (mxq(f64(w1), 0, "e4m3").T @ v) * f64(gain)[:, None]
    xa = heads(h, f64(wga), unstriped8(offs2))
    xb = heads(h, f64(wgb), unstriped8(offs3))
    x = np.sin(xa + xb) * f64(amp)[:, None]
    w2 = unpack_weight(w2_words, w2_scales, "e2m1")
    y = w2.T @ mxq(x, 0, "e4m3")
    return y * xb

@@ -1,0 +1,209 @@
+from contextlib import ExitStack
+
+import concourse.mybir as mybir
+
+K, H, T, S, PAIRS = 1536, 512, 4096, 1024, 512
+FLOPS = 2 * K * H * S + 2 * H * H * PAIRS
+
+F32 = mybir.dt.float32
+BF16 = mybir.dt.bfloat16
+I32 = mybir.dt.int32
+U32 = mybir.dt.uint32
+U16 = mybir.dt.uint16
+U8 = mybir.dt.uint8
+FP8X4 = mybir.dt.float8_e4m3fn_x4
+FP4X4 = mybir.dt.float4_e2m1fn_x4
+ALU = mybir.AluOpType
+ACT = mybir.ActivationFunctionType
+
+P = 128
+PACK = 4
+PASSES = K // (P * PACK)
+BANK = 512
+HALVES = S // BANK
+CHUNKS = ((0, 256), (256, 128), (384, 128))
+
+
+def tile_list_trophallaxis_flow_scores_kernel(
+    tc, tab_words, tab_scales, offs, w1, gain, offs2, wga, offs3, wgb, amp, w2_words, w2_scales, out
+):
+    nc = tc.nc
+    with ExitStack() as ctx:
+        keep = ctx.enter_context(tc.tile_pool(name="keep", bufs=1))
+        psum = ctx.enter_context(tc.psum_pool(name="psum", bufs=1))
+
+        def sb(name, shape, dtype):
+            return keep.tile(shape, dtype, name=name, align_bytes=64)
+
+        def bank(index, name):
+            return psum.tile([P, BANK], F32, name=name, tag="bank%d" % index)
+
+        picks = sb("picks", [P, S // 16], U16)
+        donors = sb("donors", [P, PAIRS // 16], U16)
+        receivers = sb("receivers", [P, PAIRS // 16], U16)
+        table = [sb("table%d" % a, [P, T], I32) for a in range(PASSES)]
+        table_scale = sb("table_scale", [P, T], U8)
+        w1_raw = [sb("w1_raw%d" % a, [P, PACK, H], F32) for a in range(PASSES - 1)]
+        w1_last = [sb("w1_last%d" % u, [P, PACK, H // 2], F32) for u in range(2)]
+        w2_raw = sb("w2_raw", [P, 2 * H], U8)
+        w2_scale_raw = sb("w2_scale_raw", [P, H], U8)
+        gain_sb = sb("gain_sb", [P, PACK], F32)
+        amp_sb = sb("amp_sb", [P, PACK], F32)
+        wga_sb = sb("wga_sb", [P, PAIRS], F32)
+        wgb_sb = sb("wgb_sb", [P, PAIRS], F32)
+
+        nc.vector.memset(table_scale[:].bitcast(I32), 0)
+        nc.vector.memset(w2_scale_raw[:].bitcast(I32), 0)
+
+        def load_table(a):
+            nc.sync.dma_start(table[a][:], tab_words[a].rearrange("p t i -> p (t i)").bitcast(I32))
+
+        def w1_rows(a):
+            return w1[a * P * PACK : (a + 1) * P * PACK, :].rearrange("(p j) c -> p j c", j=PACK)
+
+        load_table(0)
+        nc.sync.dma_start(picks[:], offs)
+        nc.sync.dma_start(w2_raw[:].bitcast(I32), w2_words[0].bitcast(I32))
+        nc.sync.dma_start(receivers[:], offs3)
+        nc.sync.dma_start(donors[:], offs2)
+        nc.sync.dma_start(gain_sb[:], gain.rearrange("(p i) -> p i", i=PACK))
+        nc.sync.dma_start(amp_sb[:], amp.rearrange("(p i) -> p i", i=PACK))
+        load_table(1)
+        nc.sync.dma_start(w1_raw[0][:], w1_rows(0))
+        nc.sync.dma_start(w1_raw[1][:], w1_rows(1))
+        load_table(2)
+        for u in range(2):
+            nc.sync.dma_start(w1_last[u][:], w1_rows(2)[:, :, u * (H // 2) : (u + 1) * (H // 2)])
+        nc.sync.dma_start(wgb_sb[:], wgb)
+        nc.sync.dma_start(wga_sb[:], wga)
+
+        for q in range(4):
+            nc.gpsimd.dma_start(
+                table_scale[32 * q : 32 * q + 4 * PASSES, :].bitcast(I32),
+                tab_scales[:, 4 * q : 4 * q + 4, :].bitcast(I32),
+            )
+        for q in range(4):
+            nc.gpsimd.dma_start(
+                w2_scale_raw[32 * q : 32 * q + 4, :].bitcast(I32),
+                w2_scales[0, 4 * q : 4 * q + 4, :].bitcast(I32),
+            )
+
+        w2_codes = sb("w2_codes", [P, 2 * H], U8)
+        w2_scale = sb("w2_scale", [P, H], U8)
+        nc.vector.tensor_copy(
+            w2_codes[:].rearrange("p (i q b) -> p i q b", i=PACK, b=2),
+            w2_raw[:].rearrange("p (q i b) -> p i q b", i=PACK, b=2),
+        )
+        nc.vector.tensor_copy(
+            w2_scale[:].rearrange("p (i q) -> p i q", i=PACK),
+            w2_scale_raw[:].rearrange("p (q i) -> p i q", i=PACK),
+        )
+
+        v_scale = sb("v_scale", [P, S], U8)
+        v_words = [[sb("v_words%d_%d" % (a, u), [P, BANK], U32) for u in range(HALVES)] for a in range(PASSES)]
+        w1_bf = [sb("w1_bf%d" % a, [P, PACK, P, PACK], BF16) for a in range(PASSES)]
+        w1_codes = [[sb("w1_codes%d_%d" % (a, i), [P, P], U32) for i in range(PACK)] for a in range(PASSES)]
+        w1_scale = [[sb("w1_scale%d_%d" % (a, i), [P, P], U8) for i in range(PACK)] for a in range(PASSES)]
+        h_banks = [[bank(HALVES * i + u, "h_bank%d_%d" % (i, u)) for u in range(HALVES)] for i in range(PACK)]
+
+        nc.vector.tensor_copy(v_scale[:], table_scale[:].indirect(picks[:]))
+
+        for a in range(PASSES):
+            for u in range(HALVES):
+                cols = slice(u * BANK // 16, (u + 1) * BANK // 16)
+                nc.vector.tensor_copy(v_words[a][u][:], table[a][:].bitcast(U32).indirect(picks[:, cols]))
+            dealt = w1_bf[a][:].rearrange("p i q j -> p q i j")
+            if a < PASSES - 1:
+                nc.scalar.copy(dealt, w1_raw[a][:].rearrange("p j (q i) -> p q i j", i=PACK))
+            else:
+                for u in range(2):
+                    nc.vector.tensor_copy(
+                        dealt[:, u * (P // 2) : (u + 1) * (P // 2)],
+                        w1_last[u][:].rearrange("p j (q i) -> p q i j", i=PACK),
+                    )
+            for i in range(PACK):
+                nc.vector.quantize_mx(
+                    out=w1_codes[a][i][:].bitcast(FP8X4),
+                    scales=w1_scale[a][i][:],
+                    in_=w1_bf[a][:, i].rearrange("p q j -> p (q j)"),
+                )
+            for i in range(PACK):
+                for u in range(HALVES):
+                    nc.tensor.matmul_mx(
+                        out=h_banks[i][u][:],
+                        lhsT=w1_codes[a][i][:].bitcast(FP8X4),
+                        lhsT_scale=w1_scale[a][i][:],
+                        rhs=v_words[a][u][:].bitcast(FP8X4),
+                        rhs_scale=v_scale[4 * a : P, u * BANK : (u + 1) * BANK],
+                        start=(a == 0),
+                        stop=(a == PASSES - 1),
+                    )
+
+        h = [sb("h%d" % i, [P, S], F32) for i in range(PACK)]
+        for i in range(PACK):
+            for u in range(HALVES):
+                nc.scalar.activation(
+                    h[i][:, u * BANK : (u + 1) * BANK], h_banks[i][u][:], ACT.Copy, scale=gain_sb[:, i : i + 1]
+                )
+
+        out_rows = out.rearrange("(p i) m -> p i m", i=PACK)
+        xb, arg, sines, x_bf = {}, {}, {}, {}
+
+        def pick_sides(c):
+            m0, w = CHUNKS[c]
+            cols = slice(m0 // 16, (m0 + w) // 16)
+            xa = sb("xa%d" % c, [P, PACK, w], F32)
+            xb[c] = sb("xb%d" % c, [P, PACK, w], F32)
+            arg[c] = sb("arg%d" % c, [P, PACK, w], F32)
+            for i in range(PACK):
+                nc.vector.tensor_tensor(
+                    xb[c][:, i, :], h[i][:].indirect(receivers[:, cols]), wgb_sb[:, m0 : m0 + w], ALU.mult
+                )
+                nc.vector.tensor_tensor(
+                    xa[:, i, :], h[i][:].indirect(donors[:, cols]), wga_sb[:, m0 : m0 + w], ALU.mult
+                )
+            nc.vector.tensor_tensor(arg[c][:], xa[:], xb[c][:], ALU.add)
+            sines[c] = sb("sines%d" % c, [P, w, PACK], F32)
+            nc.scalar.activation(sines[c][:], arg[c][:].rearrange("p i m -> p m i"), ACT.Sin)
+
+        def finish(c, first_bank):
+            m0, w = CHUNKS[c]
+            x_bf[c] = sb("x_bf%d" % c, [P, w, PACK], BF16)
+            nc.vector.tensor_tensor(
+                x_bf[c][:], sines[c][:], amp_sb[:].unsqueeze(1).to_broadcast([P, w, PACK]), ALU.mult
+            )
+            x_codes = sb("x_codes%d" % c, [P, w], U32)
+            x_scale = sb("x_scale%d" % c, [P, w], U8)
+            nc.vector.quantize_mx(
+                out=x_codes[:].bitcast(FP8X4), scales=x_scale[:], in_=x_bf[c][:].rearrange("p m i -> p (m i)")
+            )
+            per_bank = BANK // w
+            result = sb("result%d" % c, [P, PACK, w], F32)
+            for b in range(PACK // per_bank):
+                y = bank(first_bank + b, "y%d_%d" % (c, b))
+                for s in range(per_bank):
+                    i = b * per_bank + s
+                    nc.tensor.matmul_mx(
+                        out=y[:, s * w : (s + 1) * w],
+                        lhsT=w2_codes[:, 2 * P * i : 2 * P * (i + 1)].bitcast(FP4X4),
+                        lhsT_scale=w2_scale[:, P * i : P * (i + 1)],
+                        rhs=x_codes[:].bitcast(FP8X4),
+                        rhs_scale=x_scale[:],
+                        start=True,
+                        stop=True,
+                    )
+                rows = slice(b * per_bank, (b + 1) * per_bank)
+                nc.vector.tensor_tensor(
+                    result[:, rows, :].rearrange("p i m -> p (i m)"),
+                    y[:],
+                    xb[c][:, rows, :].rearrange("p i m -> p (i m)"),
+                    ALU.mult,
+                )
+            nc.sync.dma_start(out_rows[:, :, m0 : m0 + w], result[:])
+
+        pick_sides(0)
+        pick_sides(1)
+        finish(0, 0)
+        pick_sides(2)
+        finish(1, 2)
+        finish(2, 3)

@@ -32,8 +32,8 @@ def tile_list_trophallaxis_flow_scores_kernel(
         keep = ctx.enter_context(tc.tile_pool(name="keep", bufs=1))
         psum = ctx.enter_context(tc.psum_pool(name="psum", bufs=1))
 
-        def sb(name, shape, dtype):
-            return keep.tile(shape, dtype, name=name, align_bytes=64)
+        def sb(name, shape, dtype, tag=None):
+            return keep.tile(shape, dtype, name=name, tag=tag or name, align_bytes=64)
 
         def bank(index, name):
             return psum.tile([P, BANK], F32, name=name, tag="bank%d" % index)
@@ -52,8 +52,8 @@ def tile_list_trophallaxis_flow_scores_kernel(
         wga_sb = sb("wga_sb", [P, PAIRS], F32)
         wgb_sb = sb("wgb_sb", [P, PAIRS], F32)
 
+        nc.gpsimd.memset(w2_scale_raw[:].bitcast(I32), 0)
         nc.vector.memset(table_scale[:].bitcast(I32), 0)
-        nc.vector.memset(w2_scale_raw[:].bitcast(I32), 0)
 
         def load_table(a):
             nc.sync.dma_start(table[a][:], tab_words[a].rearrange("p t i -> p (t i)").bitcast(I32))
@@ -63,30 +63,29 @@ def tile_list_trophallaxis_flow_scores_kernel(
 
         load_table(0)
         nc.sync.dma_start(picks[:], offs)
-        nc.sync.dma_start(w2_raw[:].bitcast(I32), w2_words[0].bitcast(I32))
-        nc.sync.dma_start(receivers[:], offs3)
-        nc.sync.dma_start(donors[:], offs2)
-        nc.sync.dma_start(gain_sb[:], gain.rearrange("(p i) -> p i", i=PACK))
-        nc.sync.dma_start(amp_sb[:], amp.rearrange("(p i) -> p i", i=PACK))
-        load_table(1)
-        nc.sync.dma_start(w1_raw[0][:], w1_rows(0))
-        nc.sync.dma_start(w1_raw[1][:], w1_rows(1))
-        load_table(2)
-        for u in range(2):
-            nc.sync.dma_start(w1_last[u][:], w1_rows(2)[:, :, u * (H // 2) : (u + 1) * (H // 2)])
-        nc.sync.dma_start(wgb_sb[:], wgb)
-        nc.sync.dma_start(wga_sb[:], wga)
-
         for q in range(4):
-            nc.gpsimd.dma_start(
-                table_scale[32 * q : 32 * q + 4 * PASSES, :].bitcast(I32),
-                tab_scales[:, 4 * q : 4 * q + 4, :].bitcast(I32),
-            )
-        for q in range(4):
-            nc.gpsimd.dma_start(
+            nc.sync.dma_start(
                 w2_scale_raw[32 * q : 32 * q + 4, :].bitcast(I32),
                 w2_scales[0, 4 * q : 4 * q + 4, :].bitcast(I32),
             )
+        nc.sync.dma_start(w2_raw[:].bitcast(I32), w2_words[0].bitcast(I32))
+        load_table(1)
+        for q in range(4):
+            nc.sync.dma_start(
+                table_scale[32 * q : 32 * q + 4 * PASSES, :].bitcast(I32),
+                tab_scales[:, 4 * q : 4 * q + 4, :].bitcast(I32),
+            )
+        nc.sync.dma_start(w1_raw[0][:], w1_rows(0))
+        nc.sync.dma_start(w1_raw[1][:], w1_rows(1))
+        load_table(2)
+        nc.sync.dma_start(gain_sb[:], gain.rearrange("(p i) -> p i", i=PACK))
+        for u in range(2):
+            nc.sync.dma_start(w1_last[u][:], w1_rows(2)[:, :, u * (H // 2) : (u + 1) * (H // 2)])
+        nc.sync.dma_start(receivers[:], offs3)
+        nc.sync.dma_start(wgb_sb[:], wgb)
+        nc.sync.dma_start(donors[:], offs2)
+        nc.sync.dma_start(wga_sb[:], wga)
+        nc.sync.dma_start(amp_sb[:], amp.rearrange("(p i) -> p i", i=PACK))
 
         w2_codes = sb("w2_codes", [P, 2 * H], U8)
         w2_scale = sb("w2_scale", [P, H], U8)
@@ -117,7 +116,8 @@ def tile_list_trophallaxis_flow_scores_kernel(
                 nc.scalar.copy(dealt, w1_raw[a][:].rearrange("p j (q i) -> p q i j", i=PACK))
             else:
                 for u in range(2):
-                    nc.vector.tensor_copy(
+                    cast = nc.vector.tensor_copy if u else nc.scalar.copy
+                    cast(
                         dealt[:, u * (P // 2) : (u + 1) * (P // 2)],
                         w1_last[u][:].rearrange("p j (q i) -> p q i j", i=PACK),
                     )
@@ -142,68 +142,112 @@ def tile_list_trophallaxis_flow_scores_kernel(
         h = [sb("h%d" % i, [P, S], F32) for i in range(PACK)]
         for i in range(PACK):
             for u in range(HALVES):
-                nc.scalar.activation(
-                    h[i][:, u * BANK : (u + 1) * BANK], h_banks[i][u][:], ACT.Copy, scale=gain_sb[:, i : i + 1]
-                )
+                cols = slice(u * BANK, (u + 1) * BANK)
+                if (i, u) == (0, HALVES - 1):
+                    nc.vector.tensor_scalar(h[i][:, cols], h_banks[i][u][:], gain_sb[:, i : i + 1], None, ALU.mult)
+                else:
+                    nc.scalar.activation(h[i][:, cols], h_banks[i][u][:], ACT.Copy, scale=gain_sb[:, i : i + 1])
 
         out_rows = out.rearrange("(p i) m -> p i m", i=PACK)
-        xb, arg, sines, x_bf = {}, {}, {}, {}
 
-        def pick_sides(c):
-            m0, w = CHUNKS[c]
+        def pick(dst_a, dst_b, i, m0, w):
             cols = slice(m0 // 16, (m0 + w) // 16)
-            xa = sb("xa%d" % c, [P, PACK, w], F32)
-            xb[c] = sb("xb%d" % c, [P, PACK, w], F32)
-            arg[c] = sb("arg%d" % c, [P, PACK, w], F32)
-            for i in range(PACK):
-                nc.vector.tensor_tensor(
-                    xb[c][:, i, :], h[i][:].indirect(receivers[:, cols]), wgb_sb[:, m0 : m0 + w], ALU.mult
-                )
-                nc.vector.tensor_tensor(
-                    xa[:, i, :], h[i][:].indirect(donors[:, cols]), wga_sb[:, m0 : m0 + w], ALU.mult
-                )
-            nc.vector.tensor_tensor(arg[c][:], xa[:], xb[c][:], ALU.add)
-            sines[c] = sb("sines%d" % c, [P, w, PACK], F32)
-            nc.scalar.activation(sines[c][:], arg[c][:].rearrange("p i m -> p m i"), ACT.Sin)
+            nc.vector.tensor_tensor(dst_b, h[i][:].indirect(receivers[:, cols]), wgb_sb[:, m0 : m0 + w], ALU.mult)
+            nc.vector.tensor_tensor(dst_a, h[i][:].indirect(donors[:, cols]), wga_sb[:, m0 : m0 + w], ALU.mult)
 
-        def finish(c, first_bank):
-            m0, w = CHUNKS[c]
-            x_bf[c] = sb("x_bf%d" % c, [P, w, PACK], BF16)
-            nc.vector.tensor_tensor(
-                x_bf[c][:], sines[c][:], amp_sb[:].unsqueeze(1).to_broadcast([P, w, PACK]), ALU.mult
-            )
+        def activate(xa, xb, arg, sines, x_rows, first):
+            nc.vector.tensor_tensor(arg, xa, xb, ALU.add)
+            nc.scalar.activation(sines, arg, ACT.Sin)
+            for s in range(x_rows.shape[1]):
+                i = first + s
+                nc.scalar.activation(x_rows[:, s, :], sines[:, s, :], ACT.Copy, scale=amp_sb[:, i : i + 1])
+
+        def quantize_x(c, x_bf):
+            w = x_bf.shape[1]
             x_codes = sb("x_codes%d" % c, [P, w], U32)
             x_scale = sb("x_scale%d" % c, [P, w], U8)
             nc.vector.quantize_mx(
-                out=x_codes[:].bitcast(FP8X4), scales=x_scale[:], in_=x_bf[c][:].rearrange("p m i -> p (m i)")
+                out=x_codes[:].bitcast(FP8X4), scales=x_scale[:], in_=x_bf[:].rearrange("p m i -> p (m i)")
             )
-            per_bank = BANK // w
-            result = sb("result%d" % c, [P, PACK, w], F32)
-            for b in range(PACK // per_bank):
-                y = bank(first_bank + b, "y%d_%d" % (c, b))
-                for s in range(per_bank):
-                    i = b * per_bank + s
-                    nc.tensor.matmul_mx(
-                        out=y[:, s * w : (s + 1) * w],
-                        lhsT=w2_codes[:, 2 * P * i : 2 * P * (i + 1)].bitcast(FP4X4),
-                        lhsT_scale=w2_scale[:, P * i : P * (i + 1)],
-                        rhs=x_codes[:].bitcast(FP8X4),
-                        rhs_scale=x_scale[:],
-                        start=True,
-                        stop=True,
-                    )
-                rows = slice(b * per_bank, (b + 1) * per_bank)
-                nc.vector.tensor_tensor(
-                    result[:, rows, :].rearrange("p i m -> p (i m)"),
-                    y[:],
-                    xb[c][:, rows, :].rearrange("p i m -> p (i m)"),
-                    ALU.mult,
-                )
-            nc.sync.dma_start(out_rows[:, :, m0 : m0 + w], result[:])
+            return x_codes, x_scale
 
-        pick_sides(0)
-        pick_sides(1)
-        finish(0, 0)
-        pick_sides(2)
-        finish(1, 2)
-        finish(2, 3)
+        def mix(name, bank_index, x_quantized, first, count):
+            x_codes, x_scale = x_quantized
+            w = x_codes.shape[1]
+            y = bank(bank_index, name)
+            for s in range(count):
+                i = first + s
+                nc.tensor.matmul_mx(
+                    out=y[:, s * w : (s + 1) * w],
+                    lhsT=w2_codes[:, 2 * P * i : 2 * P * (i + 1)].bitcast(FP4X4),
+                    lhsT_scale=w2_scale[:, P * i : P * (i + 1)],
+                    rhs=x_codes[:].bitcast(FP8X4),
+                    rhs_scale=x_scale[:],
+                    start=True,
+                    stop=True,
+                )
+            return y[:, 0 : count * w].rearrange("p (i m) -> p i m", i=count)
+
+        def weigh(name, y, xb):
+            result = sb(name, list(y.shape), F32)
+            nc.vector.tensor_tensor(result[:], y, xb, ALU.mult)
+            return result
+
+        (m0, w0), (m1, w1c), (m2, w2c) = CHUNKS
+
+        xa0 = sb("xa0", [P, PACK, w0], F32, "after_sum0")
+        xb0 = sb("xb0", [P, PACK, w0], F32)
+        arg0 = sb("arg0", [P, PACK, w0], F32, "after_sine0")
+        sines0 = sb("sines0", [P, PACK, w0], F32)
+        x_rows0 = sb("x_rows0", [P, PACK, w0], BF16)
+        x_bf0 = sb("x_bf0", [P, w0, PACK], BF16, "after_quantize0")
+        for i in range(PACK):
+            pick(xa0[:, i, :], xb0[:, i, :], i, m0, w0)
+        activate(xa0[:], xb0[:], arg0[:], sines0[:], x_rows0[:], 0)
+        nc.scalar.copy(x_bf0[:], x_rows0[:].rearrange("p i m -> p m i"))
+
+        sides1 = sb("sides1", [P, 2, PACK, w1c], F32, "after_sum0")
+        arg1 = sb("arg1", [P, PACK, w1c], F32)
+        sines1 = sb("sines1", [P, PACK, w1c], F32)
+        x_rows1 = sb("x_rows1", [P, PACK, w1c], BF16)
+        x_bf1 = sb("x_bf1", [P, w1c, PACK], BF16)
+        for i in range(PACK):
+            pick(sides1[:, 0, i, :], sides1[:, 1, i, :], i, m1, w1c)
+        activate(sides1[:, 0], sides1[:, 1], arg1[:], sines1[:], x_rows1[:], 0)
+        nc.scalar.copy(x_bf1[:], x_rows1[:].rearrange("p i m -> p m i"))
+
+        arg2 = sb("arg2", [P, PACK, w2c], F32)
+        sines2 = sb("sines2", [P, PACK, w2c], F32)
+        x_rows2 = sb("x_rows2", [P, PACK, w2c], BF16)
+        x_bf2 = sb("x_bf2", [P, w2c, PACK], BF16)
+        sides2_low = sb("sides2_low", [P, 2, 2, w2c], F32, "after_sine0")
+        for i in range(2):
+            pick(sides2_low[:, 0, i, :], sides2_low[:, 1, i, :], i, m2, w2c)
+        activate(sides2_low[:, 0], sides2_low[:, 1], arg2[:, 0:2], sines2[:, 0:2], x_rows2[:, 0:2], 0)
+
+        x0 = quantize_x(0, x_bf0)
+        y0 = [mix("y0_%d" % b, b, x0, 2 * b, 2) for b in range(2)]
+
+        sides2_high = sb("sides2_high", [P, 2, 2, w2c], F32, "after_quantize0")
+        for i in range(2, PACK):
+            pick(sides2_high[:, 0, i - 2, :], sides2_high[:, 1, i - 2, :], i, m2, w2c)
+            rows = slice(i, i + 1)
+            local = slice(i - 2, i - 1)
+            activate(
+                sides2_high[:, 0, local], sides2_high[:, 1, local], arg2[:, rows], sines2[:, rows], x_rows2[:, rows], i
+            )
+
+        x1 = quantize_x(1, x_bf1)
+        y1 = mix("y1", 2, x1, 0, PACK)
+        for b in range(2):
+            result = weigh("result0_%d" % b, y0[b], xb0[:, 2 * b : 2 * b + 2])
+            nc.sync.dma_start(out_rows[:, 2 * b : 2 * b + 2, m0 : m0 + w0], result[:])
+
+        nc.vector.tensor_copy(x_bf2[:], x_rows2[:].rearrange("p i m -> p m i"))
+        x2 = quantize_x(2, x_bf2)
+        y2 = [mix("y2_%d" % b, 3 + b, x2, 2 * b, 2) for b in range(2)]
+        result = weigh("result1", y1, sides1[:, 1])
+        nc.sync.dma_start(out_rows[:, :, m1 : m1 + w1c], result[:])
+        for b, sides in enumerate((sides2_low, sides2_high)):
+            result = weigh("result2_%d" % b, y2[b], sides[:, 1])
+            nc.sync.dma_start(out_rows[:, 2 * b : 2 * b + 2, m2 : m2 + w2c], result[:])

@@ -1,6 +1,7 @@
 from contextlib import ExitStack
 
 import concourse.mybir as mybir
+from concourse.masks import make_identity
 
 K, H, T, S, PAIRS = 1536, 512, 4096, 1024, 512
 FLOPS = 2 * K * H * S + 2 * H * H * PAIRS
@@ -21,6 +22,7 @@ PACK = 4
 PASSES = K // (P * PACK)
 BANK = 512
 HALVES = S // BANK
+CAST_SPLIT = 80
 CHUNKS = ((0, 256), (256, 128), (384, 128))
 
 
@@ -52,8 +54,8 @@ def tile_list_trophallaxis_flow_scores_kernel(
         wga_sb = sb("wga_sb", [P, PAIRS], F32)
         wgb_sb = sb("wgb_sb", [P, PAIRS], F32)
 
-        nc.gpsimd.memset(w2_scale_raw[:].bitcast(I32), 0)
         nc.vector.memset(table_scale[:].bitcast(I32), 0)
+        nc.vector.memset(w2_scale_raw[:].bitcast(I32), 0)
 
         def load_table(a):
             nc.sync.dma_start(table[a][:], tab_words[a].rearrange("p t i -> p (t i)").bitcast(I32))
@@ -63,35 +65,39 @@ def tile_list_trophallaxis_flow_scores_kernel(
 
         load_table(0)
         nc.sync.dma_start(picks[:], offs)
-        for q in range(4):
-            nc.sync.dma_start(
-                w2_scale_raw[32 * q : 32 * q + 4, :].bitcast(I32),
-                w2_scales[0, 4 * q : 4 * q + 4, :].bitcast(I32),
-            )
         nc.sync.dma_start(w2_raw[:].bitcast(I32), w2_words[0].bitcast(I32))
         load_table(1)
-        for q in range(4):
-            nc.sync.dma_start(
-                table_scale[32 * q : 32 * q + 4 * PASSES, :].bitcast(I32),
-                tab_scales[:, 4 * q : 4 * q + 4, :].bitcast(I32),
-            )
         nc.sync.dma_start(w1_raw[0][:], w1_rows(0))
         nc.sync.dma_start(w1_raw[1][:], w1_rows(1))
         load_table(2)
-        nc.sync.dma_start(gain_sb[:], gain.rearrange("(p i) -> p i", i=PACK))
         for u in range(2):
             nc.sync.dma_start(w1_last[u][:], w1_rows(2)[:, :, u * (H // 2) : (u + 1) * (H // 2)])
+        nc.sync.dma_start(gain_sb[:], gain.rearrange("(p i) -> p i", i=PACK))
         nc.sync.dma_start(receivers[:], offs3)
         nc.sync.dma_start(wgb_sb[:], wgb)
         nc.sync.dma_start(donors[:], offs2)
         nc.sync.dma_start(wga_sb[:], wga)
         nc.sync.dma_start(amp_sb[:], amp.rearrange("(p i) -> p i", i=PACK))
 
+        for q in range(4):
+            nc.gpsimd.dma_start(
+                table_scale[32 * q : 32 * q + 4 * PASSES, :].bitcast(I32),
+                tab_scales[:, 4 * q : 4 * q + 4, :].bitcast(I32),
+            )
+        for q in range(4):
+            nc.gpsimd.dma_start(
+                w2_scale_raw[32 * q : 32 * q + 4, :].bitcast(I32),
+                w2_scales[0, 4 * q : 4 * q + 4, :].bitcast(I32),
+            )
+
+        identity = sb("identity", [P, P], F32)
+        make_identity(nc, identity[:])
+
         w2_codes = sb("w2_codes", [P, 2 * H], U8)
         w2_scale = sb("w2_scale", [P, H], U8)
         nc.vector.tensor_copy(
-            w2_codes[:].rearrange("p (i q b) -> p i q b", i=PACK, b=2),
-            w2_raw[:].rearrange("p (q i b) -> p i q b", i=PACK, b=2),
+            w2_codes[:].bitcast(U16).rearrange("p (i q) -> p i q", i=PACK),
+            w2_raw[:].bitcast(U16).rearrange("p (q i) -> p i q", i=PACK),
         )
         nc.vector.tensor_copy(
             w2_scale[:].rearrange("p (i q) -> p i q", i=PACK),
@@ -113,14 +119,15 @@ def tile_list_trophallaxis_flow_scores_kernel(
                 nc.vector.tensor_copy(v_words[a][u][:], table[a][:].bitcast(U32).indirect(picks[:, cols]))
             dealt = w1_bf[a][:].rearrange("p i q j -> p q i j")
             if a < PASSES - 1:
-                nc.scalar.copy(dealt, w1_raw[a][:].rearrange("p j (q i) -> p q i j", i=PACK))
+                rows = w1_raw[a][:].rearrange("p j (q i) -> p q i j", i=PACK)
+                nc.vector.tensor_copy(dealt[:, 0:CAST_SPLIT], rows[:, 0:CAST_SPLIT])
+                nc.scalar.copy(dealt[:, CAST_SPLIT:P], rows[:, CAST_SPLIT:P])
             else:
                 for u in range(2):
-                    cast = nc.vector.tensor_copy if u else nc.scalar.copy
-                    cast(
-                        dealt[:, u * (P // 2) : (u + 1) * (P // 2)],
-                        w1_last[u][:].rearrange("p j (q i) -> p q i j", i=PACK),
-                    )
+                    rows = w1_last[u][:].rearrange("p j (q i) -> p q i j", i=PACK)
+                    half = dealt[:, u * (P // 2) : (u + 1) * (P // 2)]
+                    nc.vector.tensor_copy(half[:, :, 0:2], rows[:, :, 0:2])
+                    nc.scalar.copy(half[:, :, 2:PACK], rows[:, :, 2:PACK])
             for i in range(PACK):
                 nc.vector.quantize_mx(
                     out=w1_codes[a][i][:].bitcast(FP8X4),
@@ -162,6 +169,29 @@ def tile_list_trophallaxis_flow_scores_kernel(
                 i = first + s
                 nc.scalar.activation(x_rows[:, s, :], sines[:, s, :], ACT.Copy, scale=amp_sb[:, i : i + 1])
 
+        def activate_turned(name, banks, xa, xb, x_rows, first):
+            count, w = xa.shape[1], xa.shape[2]
+            blocks = [(s, b) for s in range(count) for b in range(w // P)]
+            turned = bank(banks[0], name + "_turned")
+            for n, (s, b) in enumerate(blocks):
+                for side, last in ((xb, False), (xa, True)):
+                    nc.tensor.matmul(
+                        turned[:, n * P : (n + 1) * P],
+                        side[:, s, b * P : (b + 1) * P],
+                        identity[:],
+                        start=not last,
+                        stop=last,
+                        is_transpose=True,
+                    )
+            sines = sb(name + "_sines", [P, count * w], F32)
+            nc.scalar.activation(sines[:], turned[:, 0 : count * w], ACT.Sin)
+            back = bank(banks[1], name + "_back")
+            for n in range(len(blocks)):
+                nc.tensor.transpose(back[:, n * P : (n + 1) * P], sines[:, n * P : (n + 1) * P], identity[:])
+            for s in range(count):
+                i = first + s
+                nc.scalar.activation(x_rows[:, s, :], back[:, s * w : (s + 1) * w], ACT.Copy, scale=amp_sb[:, i : i + 1])
+
         def quantize_x(c, x_bf):
             w = x_bf.shape[1]
             x_codes = sb("x_codes%d" % c, [P, w], U32)
@@ -195,25 +225,31 @@ def tile_list_trophallaxis_flow_scores_kernel(
 
         (m0, w0), (m1, w1c), (m2, w2c) = CHUNKS
 
-        xa0 = sb("xa0", [P, PACK, w0], F32, "after_sum0")
+        last = PACK - 1
+        xa0 = sb("xa0", [P, last, w0], F32)
+        xa0_last = sb("xa0_last", [P, 1, w0], F32, "after_sum0")
         xb0 = sb("xb0", [P, PACK, w0], F32)
-        arg0 = sb("arg0", [P, PACK, w0], F32, "after_sine0")
-        sines0 = sb("sines0", [P, PACK, w0], F32)
+        arg0 = sb("arg0", [P, 1, w0], F32, "after_sine0")
+        sines0 = sb("sines0", [P, 1, w0], F32)
         x_rows0 = sb("x_rows0", [P, PACK, w0], BF16)
         x_bf0 = sb("x_bf0", [P, w0, PACK], BF16, "after_quantize0")
-        for i in range(PACK):
+        for i in range(last):
             pick(xa0[:, i, :], xb0[:, i, :], i, m0, w0)
-        activate(xa0[:], xb0[:], arg0[:], sines0[:], x_rows0[:], 0)
+        pick(xa0_last[:, 0, :], xb0[:, last, :], last, m0, w0)
+        activate_turned("low0", (0, 2), xa0[:, 0:2], xb0[:, 0:2], x_rows0[:, 0:2], 0)
+        activate_turned("mid0", (1, 3), xa0[:, 2:last], xb0[:, 2:last], x_rows0[:, 2:last], 2)
+        activate(xa0_last[:], xb0[:, last:PACK], arg0[:], sines0[:], x_rows0[:, last:PACK], last)
         nc.scalar.copy(x_bf0[:], x_rows0[:].rearrange("p i m -> p m i"))
 
         sides1 = sb("sides1", [P, 2, PACK, w1c], F32, "after_sum0")
-        arg1 = sb("arg1", [P, PACK, w1c], F32)
-        sines1 = sb("sines1", [P, PACK, w1c], F32)
+        arg1 = sb("arg1", [P, 1, w1c], F32)
+        sines1 = sb("sines1", [P, 1, w1c], F32)
         x_rows1 = sb("x_rows1", [P, PACK, w1c], BF16)
         x_bf1 = sb("x_bf1", [P, w1c, PACK], BF16)
         for i in range(PACK):
             pick(sides1[:, 0, i, :], sides1[:, 1, i, :], i, m1, w1c)
-        activate(sides1[:, 0], sides1[:, 1], arg1[:], sines1[:], x_rows1[:], 0)
+        activate_turned("low1", (4, 5), sides1[:, 0, 0:last], sides1[:, 1, 0:last], x_rows1[:, 0:last], 0)
+        activate(sides1[:, 0, last:PACK], sides1[:, 1, last:PACK], arg1[:], sines1[:], x_rows1[:, last:PACK], last)
         nc.scalar.copy(x_bf1[:], x_rows1[:].rearrange("p i m -> p m i"))
 
         arg2 = sb("arg2", [P, PACK, w2c], F32)
@@ -226,7 +262,7 @@ def tile_list_trophallaxis_flow_scores_kernel(
         activate(sides2_low[:, 0], sides2_low[:, 1], arg2[:, 0:2], sines2[:, 0:2], x_rows2[:, 0:2], 0)
 
         x0 = quantize_x(0, x_bf0)
-        y0 = [mix("y0_%d" % b, b, x0, 2 * b, 2) for b in range(2)]
+        y0 = [mix("y0_%d" % b, 6 + b, x0, 2 * b, 2) for b in range(2)]
 
         sides2_high = sb("sides2_high", [P, 2, 2, w2c], F32, "after_quantize0")
         for i in range(2, PACK):
@@ -238,14 +274,15 @@ def tile_list_trophallaxis_flow_scores_kernel(
             )
 
         x1 = quantize_x(1, x_bf1)
-        y1 = mix("y1", 2, x1, 0, PACK)
-        for b in range(2):
-            result = weigh("result0_%d" % b, y0[b], xb0[:, 2 * b : 2 * b + 2])
-            nc.sync.dma_start(out_rows[:, 2 * b : 2 * b + 2, m0 : m0 + w0], result[:])
+        y1 = mix("y1", 0, x1, 0, PACK)
+        result = weigh("result0_0", y0[0], xb0[:, 0:2])
+        nc.sync.dma_start(out_rows[:, 0:2, m0 : m0 + w0], result[:])
 
         nc.vector.tensor_copy(x_bf2[:], x_rows2[:].rearrange("p i m -> p m i"))
         x2 = quantize_x(2, x_bf2)
-        y2 = [mix("y2_%d" % b, 3 + b, x2, 2 * b, 2) for b in range(2)]
+        y2 = [mix("y2_%d" % b, 1 + b, x2, 2 * b, 2) for b in range(2)]
+        result = weigh("result0_1", y0[1], xb0[:, 2:PACK])
+        nc.sync.dma_start(out_rows[:, 2:PACK, m0 : m0 + w0], result[:])
         result = weigh("result1", y1, sides1[:, 1])
         nc.sync.dma_start(out_rows[:, :, m1 : m1 + w1c], result[:])
         for b, sides in enumerate((sides2_low, sides2_high)):

@@ -19,9 +19,14 @@ ACT = mybir.ActivationFunctionType
 
 P = 128
 PACK = 4
+LAST = PACK - 1
 PASSES = K // (P * PACK)
 BANK = 512
 HALVES = S // BANK
+LIST_ROWS = 16
+QUADRANTS = 4
+QUADRANT = P // QUADRANTS
+SCALE_ROWS = 4
 CAST_SPLIT = 80
 CHUNKS = ((0, 256), (256, 128), (384, 128))
 
@@ -40,9 +45,9 @@ def tile_list_trophallaxis_flow_scores_kernel(
         def bank(index, name):
             return psum.tile([P, BANK], F32, name=name, tag="bank%d" % index)
 
-        picks = sb("picks", [P, S // 16], U16)
-        donors = sb("donors", [P, PAIRS // 16], U16)
-        receivers = sb("receivers", [P, PAIRS // 16], U16)
+        picks = sb("picks", [P, S // LIST_ROWS], U16)
+        donors = sb("donors", [P, PAIRS // LIST_ROWS], U16)
+        receivers = sb("receivers", [P, PAIRS // LIST_ROWS], U16)
         table = [sb("table%d" % a, [P, T], I32) for a in range(PASSES)]
         table_scale = sb("table_scale", [P, T], U8)
         w1_raw = [sb("w1_raw%d" % a, [P, PACK, H], F32) for a in range(PASSES - 1)]
@@ -58,7 +63,7 @@ def tile_list_trophallaxis_flow_scores_kernel(
         nc.vector.memset(w2_scale_raw[:].bitcast(I32), 0)
 
         def load_table(a):
-            nc.sync.dma_start(table[a][:], tab_words[a].rearrange("p t i -> p (t i)").bitcast(I32))
+            nc.sync.dma_start(table[a][:], tab_words[a].rearrange("p t j -> p (t j)").bitcast(I32))
 
         def w1_rows(a):
             return w1[a * P * PACK : (a + 1) * P * PACK, :].rearrange("(p j) c -> p j c", j=PACK)
@@ -71,7 +76,7 @@ def tile_list_trophallaxis_flow_scores_kernel(
         nc.sync.dma_start(w1_raw[1][:], w1_rows(1))
         load_table(2)
         for u in range(2):
-            nc.sync.dma_start(w1_last[u][:], w1_rows(2)[:, :, u * (H // 2) : (u + 1) * (H // 2)])
+            nc.sync.dma_start(w1_last[u][:], w1_rows(PASSES - 1)[:, :, u * (H // 2) : (u + 1) * (H // 2)])
         nc.sync.dma_start(gain_sb[:], gain.rearrange("(p i) -> p i", i=PACK))
         nc.sync.dma_start(receivers[:], offs3)
         nc.sync.dma_start(wgb_sb[:], wgb)
@@ -79,19 +84,24 @@ def tile_list_trophallaxis_flow_scores_kernel(
         nc.sync.dma_start(wga_sb[:], wga)
         nc.sync.dma_start(amp_sb[:], amp.rearrange("(p i) -> p i", i=PACK))
 
-        for q in range(4):
+        for quad in range(QUADRANTS):
+            rows = slice(SCALE_ROWS * quad, SCALE_ROWS * (quad + 1))
             nc.gpsimd.dma_start(
-                table_scale[32 * q : 32 * q + 4 * PASSES, :].bitcast(I32),
-                tab_scales[:, 4 * q : 4 * q + 4, :].bitcast(I32),
+                table_scale[QUADRANT * quad : QUADRANT * quad + SCALE_ROWS * PASSES, :].bitcast(I32),
+                tab_scales[:, rows, :].bitcast(I32),
             )
-        for q in range(4):
+        for quad in range(QUADRANTS):
+            rows = slice(SCALE_ROWS * quad, SCALE_ROWS * (quad + 1))
             nc.gpsimd.dma_start(
-                w2_scale_raw[32 * q : 32 * q + 4, :].bitcast(I32),
-                w2_scales[0, 4 * q : 4 * q + 4, :].bitcast(I32),
+                w2_scale_raw[QUADRANT * quad : QUADRANT * quad + SCALE_ROWS, :].bitcast(I32),
+                w2_scales[0, rows, :].bitcast(I32),
             )
 
         identity = sb("identity", [P, P], F32)
         make_identity(nc, identity[:])
+
+        v_scale = sb("v_scale", [P, S], U8)
+        nc.vector.tensor_copy(v_scale[:], table_scale[:].indirect(picks[:]))
 
         w2_codes = sb("w2_codes", [P, 2 * H], U8)
         w2_scale = sb("w2_scale", [P, H], U8)
@@ -104,30 +114,26 @@ def tile_list_trophallaxis_flow_scores_kernel(
             w2_scale_raw[:].rearrange("p (q i) -> p i q", i=PACK),
         )
 
-        v_scale = sb("v_scale", [P, S], U8)
         v_words = [[sb("v_words%d_%d" % (a, u), [P, BANK], U32) for u in range(HALVES)] for a in range(PASSES)]
         w1_bf = [sb("w1_bf%d" % a, [P, PACK, P, PACK], BF16) for a in range(PASSES)]
         w1_codes = [[sb("w1_codes%d_%d" % (a, i), [P, P], U32) for i in range(PACK)] for a in range(PASSES)]
         w1_scale = [[sb("w1_scale%d_%d" % (a, i), [P, P], U8) for i in range(PACK)] for a in range(PASSES)]
         h_banks = [[bank(HALVES * i + u, "h_bank%d_%d" % (i, u)) for u in range(HALVES)] for i in range(PACK)]
 
-        nc.vector.tensor_copy(v_scale[:], table_scale[:].indirect(picks[:]))
-
         for a in range(PASSES):
             for u in range(HALVES):
-                cols = slice(u * BANK // 16, (u + 1) * BANK // 16)
-                nc.vector.tensor_copy(v_words[a][u][:], table[a][:].bitcast(U32).indirect(picks[:, cols]))
+                entries = picks[:, u * BANK // LIST_ROWS : (u + 1) * BANK // LIST_ROWS]
+                nc.vector.tensor_copy(v_words[a][u][:], table[a][:].bitcast(U32).indirect(entries))
             dealt = w1_bf[a][:].rearrange("p i q j -> p q i j")
             if a < PASSES - 1:
-                rows = w1_raw[a][:].rearrange("p j (q i) -> p q i j", i=PACK)
-                nc.vector.tensor_copy(dealt[:, 0:CAST_SPLIT], rows[:, 0:CAST_SPLIT])
-                nc.scalar.copy(dealt[:, CAST_SPLIT:P], rows[:, CAST_SPLIT:P])
+                loaded = w1_raw[a][:].rearrange("p j (q i) -> p q i j", i=PACK)
+                nc.vector.tensor_copy(dealt[:, 0:CAST_SPLIT], loaded[:, 0:CAST_SPLIT])
+                nc.scalar.copy(dealt[:, CAST_SPLIT:P], loaded[:, CAST_SPLIT:P])
             else:
-                for u in range(2):
-                    rows = w1_last[u][:].rearrange("p j (q i) -> p q i j", i=PACK)
-                    half = dealt[:, u * (P // 2) : (u + 1) * (P // 2)]
-                    nc.vector.tensor_copy(half[:, :, 0:2], rows[:, :, 0:2])
-                    nc.scalar.copy(half[:, :, 2:PACK], rows[:, :, 2:PACK])
+                early, late = (piece[:].rearrange("p j (q i) -> p q i j", i=PACK) for piece in w1_last)
+                nc.scalar.copy(dealt[:, 0 : P // 2], early)
+                nc.vector.tensor_copy(dealt[:, P // 2 : P, 0], late[:, :, 0])
+                nc.scalar.copy(dealt[:, P // 2 : P, 1:PACK], late[:, :, 1:PACK])
             for i in range(PACK):
                 nc.vector.quantize_mx(
                     out=w1_codes[a][i][:].bitcast(FP8X4),
@@ -141,7 +147,7 @@ def tile_list_trophallaxis_flow_scores_kernel(
                         lhsT=w1_codes[a][i][:].bitcast(FP8X4),
                         lhsT_scale=w1_scale[a][i][:],
                         rhs=v_words[a][u][:].bitcast(FP8X4),
-                        rhs_scale=v_scale[4 * a : P, u * BANK : (u + 1) * BANK],
+                        rhs_scale=v_scale[SCALE_ROWS * a : P, u * BANK : (u + 1) * BANK],
                         start=(a == 0),
                         stop=(a == PASSES - 1),
                     )
@@ -155,47 +161,53 @@ def tile_list_trophallaxis_flow_scores_kernel(
                 else:
                     nc.scalar.activation(h[i][:, cols], h_banks[i][u][:], ACT.Copy, scale=gain_sb[:, i : i + 1])
 
-        out_rows = out.rearrange("(p i) m -> p i m", i=PACK)
+        out_planes = out.rearrange("(p i) m -> p i m", i=PACK)
 
-        def pick(dst_a, dst_b, i, m0, w):
-            cols = slice(m0 // 16, (m0 + w) // 16)
-            nc.vector.tensor_tensor(dst_b, h[i][:].indirect(receivers[:, cols]), wgb_sb[:, m0 : m0 + w], ALU.mult)
-            nc.vector.tensor_tensor(dst_a, h[i][:].indirect(donors[:, cols]), wga_sb[:, m0 : m0 + w], ALU.mult)
+        def pick(xa, xb, i, chunk):
+            start, width = chunk
+            entries = slice(start // LIST_ROWS, (start + width) // LIST_ROWS)
+            pairs = slice(start, start + width)
+            nc.vector.tensor_tensor(xb, h[i][:].indirect(receivers[:, entries]), wgb_sb[:, pairs], ALU.mult)
+            nc.vector.tensor_tensor(xa, h[i][:].indirect(donors[:, entries]), wga_sb[:, pairs], ALU.mult)
 
-        def activate(xa, xb, arg, sines, x_rows, first):
-            nc.vector.tensor_tensor(arg, xa, xb, ALU.add)
-            nc.scalar.activation(sines, arg, ACT.Sin)
-            for s in range(x_rows.shape[1]):
+        def scale_by_amp(x_planes, sines, first):
+            for s in range(x_planes.shape[1]):
                 i = first + s
-                nc.scalar.activation(x_rows[:, s, :], sines[:, s, :], ACT.Copy, scale=amp_sb[:, i : i + 1])
+                nc.scalar.activation(x_planes[:, s, :], sines[:, s, :], ACT.Copy, scale=amp_sb[:, i : i + 1])
 
-        def activate_turned(name, banks, xa, xb, x_rows, first):
-            count, w = xa.shape[1], xa.shape[2]
-            blocks = [(s, b) for s in range(count) for b in range(w // P)]
+        def activate(xa, xb, total, sines, x_planes, first):
+            nc.vector.tensor_tensor(total, xa, xb, ALU.add)
+            nc.scalar.activation(sines, total, ACT.Sin)
+            scale_by_amp(x_planes, sines, first)
+
+        def activate_turned(name, banks, xa, xb, x_planes, first):
+            count, width = xa.shape[1], xa.shape[2]
+            blocks = [(s, b) for s in range(count) for b in range(width // P)]
             turned = bank(banks[0], name + "_turned")
             for n, (s, b) in enumerate(blocks):
-                for side, last in ((xb, False), (xa, True)):
+                for side, closes in ((xb, False), (xa, True)):
                     nc.tensor.matmul(
                         turned[:, n * P : (n + 1) * P],
                         side[:, s, b * P : (b + 1) * P],
                         identity[:],
-                        start=not last,
-                        stop=last,
+                        start=not closes,
+                        stop=closes,
                         is_transpose=True,
                     )
-            sines = sb(name + "_sines", [P, count * w], F32)
-            nc.scalar.activation(sines[:], turned[:, 0 : count * w], ACT.Sin)
+            turned_sines = sb(name + "_sines", [P, count * width], F32)
+            nc.scalar.activation(turned_sines[:], turned[:, 0 : count * width], ACT.Sin)
             back = bank(banks[1], name + "_back")
             for n in range(len(blocks)):
-                nc.tensor.transpose(back[:, n * P : (n + 1) * P], sines[:, n * P : (n + 1) * P], identity[:])
-            for s in range(count):
-                i = first + s
-                nc.scalar.activation(x_rows[:, s, :], back[:, s * w : (s + 1) * w], ACT.Copy, scale=amp_sb[:, i : i + 1])
+                nc.tensor.transpose(back[:, n * P : (n + 1) * P], turned_sines[:, n * P : (n + 1) * P], identity[:])
+            scale_by_amp(x_planes, back[:, 0 : count * width].rearrange("p (s m) -> p s m", s=count), first)
 
-        def quantize_x(c, x_bf):
-            w = x_bf.shape[1]
-            x_codes = sb("x_codes%d" % c, [P, w], U32)
-            x_scale = sb("x_scale%d" % c, [P, w], U8)
+        def interleave(x_bf, x_planes):
+            nc.scalar.copy(x_bf[:], x_planes[:].rearrange("p i m -> p m i"))
+
+        def quantize_x(name, x_bf):
+            width = x_bf.shape[1]
+            x_codes = sb(name + "_codes", [P, width], U32)
+            x_scale = sb(name + "_scale", [P, width], U8)
             nc.vector.quantize_mx(
                 out=x_codes[:].bitcast(FP8X4), scales=x_scale[:], in_=x_bf[:].rearrange("p m i -> p (m i)")
             )
@@ -203,12 +215,12 @@ def tile_list_trophallaxis_flow_scores_kernel(
 
         def mix(name, bank_index, x_quantized, first, count):
             x_codes, x_scale = x_quantized
-            w = x_codes.shape[1]
+            width = x_codes.shape[1]
             y = bank(bank_index, name)
             for s in range(count):
                 i = first + s
                 nc.tensor.matmul_mx(
-                    out=y[:, s * w : (s + 1) * w],
+                    out=y[:, s * width : (s + 1) * width],
                     lhsT=w2_codes[:, 2 * P * i : 2 * P * (i + 1)].bitcast(FP4X4),
                     lhsT_scale=w2_scale[:, P * i : P * (i + 1)],
                     rhs=x_codes[:].bitcast(FP8X4),
@@ -216,75 +228,77 @@ def tile_list_trophallaxis_flow_scores_kernel(
                     start=True,
                     stop=True,
                 )
-            return y[:, 0 : count * w].rearrange("p (i m) -> p i m", i=count)
+            return y[:, 0 : count * width].rearrange("p (i m) -> p i m", i=count)
 
-        def weigh(name, y, xb):
-            result = sb(name, list(y.shape), F32)
+        def weigh_and_store(name, y, xb, first, chunk, tag=None):
+            start, width = chunk
+            result = sb(name, list(y.shape), F32, tag)
             nc.vector.tensor_tensor(result[:], y, xb, ALU.mult)
-            return result
+            nc.sync.dma_start(out_planes[:, first : first + y.shape[1], start : start + width], result[:])
 
-        (m0, w0), (m1, w1c), (m2, w2c) = CHUNKS
+        chunk0, chunk1, chunk2 = CHUNKS
+        low, high, final = slice(0, 2), slice(2, PACK), slice(LAST, PACK)
 
-        last = PACK - 1
-        xa0 = sb("xa0", [P, last, w0], F32)
-        xa0_last = sb("xa0_last", [P, 1, w0], F32, "after_sum0")
-        xb0 = sb("xb0", [P, PACK, w0], F32)
-        arg0 = sb("arg0", [P, 1, w0], F32, "after_sine0")
-        sines0 = sb("sines0", [P, 1, w0], F32)
-        x_rows0 = sb("x_rows0", [P, PACK, w0], BF16)
-        x_bf0 = sb("x_bf0", [P, w0, PACK], BF16, "after_quantize0")
-        for i in range(last):
-            pick(xa0[:, i, :], xb0[:, i, :], i, m0, w0)
-        pick(xa0_last[:, 0, :], xb0[:, last, :], last, m0, w0)
-        activate_turned("low0", (0, 2), xa0[:, 0:2], xb0[:, 0:2], x_rows0[:, 0:2], 0)
-        activate_turned("mid0", (1, 3), xa0[:, 2:last], xb0[:, 2:last], x_rows0[:, 2:last], 2)
-        activate(xa0_last[:], xb0[:, last:PACK], arg0[:], sines0[:], x_rows0[:, last:PACK], last)
-        nc.scalar.copy(x_bf0[:], x_rows0[:].rearrange("p i m -> p m i"))
+        width = chunk0[1]
+        xa0 = sb("xa0", [P, LAST, width], F32)
+        xa0_last = sb("xa0_last", [P, 1, width], F32, "after_sum0")
+        xb0 = sb("xb0", [P, PACK, width], F32)
+        total0 = sb("total0", [P, 1, width], F32, "after_sine0")
+        sines0 = sb("sines0", [P, 1, width], F32)
+        x_planes0 = sb("x_planes0", [P, PACK, width], BF16)
+        x_bf0 = sb("x_bf0", [P, width, PACK], BF16, "after_quantize0")
+        for i in range(LAST):
+            pick(xa0[:, i, :], xb0[:, i, :], i, chunk0)
+        pick(xa0_last[:, 0, :], xb0[:, LAST, :], LAST, chunk0)
+        activate_turned("low0", (0, 2), xa0[:, low], xb0[:, low], x_planes0[:, low], 0)
+        activate_turned("mid0", (1, 3), xa0[:, 2:LAST], xb0[:, 2:LAST], x_planes0[:, 2:LAST], 2)
+        activate(xa0_last[:], xb0[:, final], total0[:], sines0[:], x_planes0[:, final], LAST)
+        interleave(x_bf0, x_planes0)
 
-        sides1 = sb("sides1", [P, 2, PACK, w1c], F32, "after_sum0")
-        arg1 = sb("arg1", [P, 1, w1c], F32)
-        sines1 = sb("sines1", [P, 1, w1c], F32)
-        x_rows1 = sb("x_rows1", [P, PACK, w1c], BF16)
-        x_bf1 = sb("x_bf1", [P, w1c, PACK], BF16)
+        width = chunk1[1]
+        sides1 = sb("sides1", [P, 2, PACK, width], F32, "after_sum0")
+        xa1, xb1 = sides1[:, 0], sides1[:, 1]
+        total1 = sb("total1", [P, 1, width], F32)
+        sines1 = sb("sines1", [P, 1, width], F32)
+        x_planes1 = sb("x_planes1", [P, PACK, width], BF16)
+        x_bf1 = sb("x_bf1", [P, width, PACK], BF16)
         for i in range(PACK):
-            pick(sides1[:, 0, i, :], sides1[:, 1, i, :], i, m1, w1c)
-        activate_turned("low1", (4, 5), sides1[:, 0, 0:last], sides1[:, 1, 0:last], x_rows1[:, 0:last], 0)
-        activate(sides1[:, 0, last:PACK], sides1[:, 1, last:PACK], arg1[:], sines1[:], x_rows1[:, last:PACK], last)
-        nc.scalar.copy(x_bf1[:], x_rows1[:].rearrange("p i m -> p m i"))
+            pick(xa1[:, i, :], xb1[:, i, :], i, chunk1)
+        activate_turned("low1", (4, 5), xa1[:, 0:LAST], xb1[:, 0:LAST], x_planes1[:, 0:LAST], 0)
+        activate(xa1[:, final], xb1[:, final], total1[:], sines1[:], x_planes1[:, final], LAST)
+        interleave(x_bf1, x_planes1)
 
-        arg2 = sb("arg2", [P, PACK, w2c], F32)
-        sines2 = sb("sines2", [P, PACK, w2c], F32)
-        x_rows2 = sb("x_rows2", [P, PACK, w2c], BF16)
-        x_bf2 = sb("x_bf2", [P, w2c, PACK], BF16)
-        sides2_low = sb("sides2_low", [P, 2, 2, w2c], F32, "after_sine0")
+        width = chunk2[1]
+        total2 = sb("total2", [P, PACK, width], F32)
+        sines2 = sb("sines2", [P, PACK, width], F32)
+        x_planes2 = sb("x_planes2", [P, PACK, width], BF16)
+        x_bf2 = sb("x_bf2", [P, width, PACK], BF16, "after_quantize2")
+        sides2_low = sb("sides2_low", [P, 2, 2, width], F32, "after_sine0")
+        xa2_low, xb2_low = sides2_low[:, 0], sides2_low[:, 1]
         for i in range(2):
-            pick(sides2_low[:, 0, i, :], sides2_low[:, 1, i, :], i, m2, w2c)
-        activate(sides2_low[:, 0], sides2_low[:, 1], arg2[:, 0:2], sines2[:, 0:2], x_rows2[:, 0:2], 0)
+            pick(xa2_low[:, i, :], xb2_low[:, i, :], i, chunk2)
+        activate(xa2_low, xb2_low, total2[:, low], sines2[:, low], x_planes2[:, low], 0)
 
-        x0 = quantize_x(0, x_bf0)
+        x0 = quantize_x("x0", x_bf0)
         y0 = [mix("y0_%d" % b, 6 + b, x0, 2 * b, 2) for b in range(2)]
 
-        sides2_high = sb("sides2_high", [P, 2, 2, w2c], F32, "after_quantize0")
-        for i in range(2, PACK):
-            pick(sides2_high[:, 0, i - 2, :], sides2_high[:, 1, i - 2, :], i, m2, w2c)
-            rows = slice(i, i + 1)
-            local = slice(i - 2, i - 1)
-            activate(
-                sides2_high[:, 0, local], sides2_high[:, 1, local], arg2[:, rows], sines2[:, rows], x_rows2[:, rows], i
-            )
+        sides2_high = sb("sides2_high", [P, 3, width], F32, "after_quantize0")
+        xa2_last = sb("xa2_last", [P, 1, width], F32, "after_last_sum")
+        xb2_high = sides2_high[:, 0:2]
+        for i, xa in ((2, sides2_high[:, 2:3]), (LAST, xa2_last[:])):
+            plane = slice(i, i + 1)
+            xb = xb2_high[:, i - 2 : i - 1]
+            pick(xa[:, 0, :], xb[:, 0, :], i, chunk2)
+            activate(xa, xb, total2[:, plane], sines2[:, plane], x_planes2[:, plane], i)
 
-        x1 = quantize_x(1, x_bf1)
+        x1 = quantize_x("x1", x_bf1)
         y1 = mix("y1", 0, x1, 0, PACK)
-        result = weigh("result0_0", y0[0], xb0[:, 0:2])
-        nc.sync.dma_start(out_rows[:, 0:2, m0 : m0 + w0], result[:])
+        weigh_and_store("result0_low", y0[0], xb0[:, low], 0, chunk0, "after_last_sum")
+        weigh_and_store("result0_high", y0[1], xb0[:, high], 2, chunk0)
 
-        nc.vector.tensor_copy(x_bf2[:], x_rows2[:].rearrange("p i m -> p m i"))
-        x2 = quantize_x(2, x_bf2)
+        interleave(x_bf2, x_planes2)
+        x2 = quantize_x("x2", x_bf2)
         y2 = [mix("y2_%d" % b, 1 + b, x2, 2 * b, 2) for b in range(2)]
-        result = weigh("result0_1", y0[1], xb0[:, 2:PACK])
-        nc.sync.dma_start(out_rows[:, 2:PACK, m0 : m0 + w0], result[:])
-        result = weigh("result1", y1, sides1[:, 1])
-        nc.sync.dma_start(out_rows[:, :, m1 : m1 + w1c], result[:])
-        for b, sides in enumerate((sides2_low, sides2_high)):
-            result = weigh("result2_%d" % b, y2[b], sides[:, 1])
-            nc.sync.dma_start(out_rows[:, 2 * b : 2 * b + 2, m2 : m2 + w2c], result[:])
+        weigh_and_store("result1", y1, xb1, 0, chunk1, "after_quantize2")
+        weigh_and_store("result2_low", y2[0], xb2_low, 0, chunk2)
+        weigh_and_store("result2_high", y2[1], xb2_high, 2, chunk2)

from contextlib import ExitStack

import concourse.mybir as mybir
from concourse.masks import make_identity

K, H, T, S, PAIRS = 1536, 512, 4096, 1024, 512
FLOPS = 2 * K * H * S + 2 * H * H * PAIRS

F32 = mybir.dt.float32
BF16 = mybir.dt.bfloat16
I32 = mybir.dt.int32
U32 = mybir.dt.uint32
U16 = mybir.dt.uint16
U8 = mybir.dt.uint8
FP8X4 = mybir.dt.float8_e4m3fn_x4
FP4X4 = mybir.dt.float4_e2m1fn_x4
ALU = mybir.AluOpType
ACT = mybir.ActivationFunctionType

P = 128
PACK = 4
LAST = PACK - 1
PASSES = K // (P * PACK)
BANK = 512
HALVES = S // BANK
LIST_ROWS = 16
QUADRANTS = 4
QUADRANT = P // QUADRANTS
SCALE_ROWS = 4
CAST_SPLIT = 80
CHUNKS = ((0, 256), (256, 128), (384, 128))


def tile_list_trophallaxis_flow_scores_kernel(
    tc, tab_words, tab_scales, offs, w1, gain, offs2, wga, offs3, wgb, amp, w2_words, w2_scales, out
):
    nc = tc.nc
    with ExitStack() as ctx:
        keep = ctx.enter_context(tc.tile_pool(name="keep", bufs=1))
        psum = ctx.enter_context(tc.psum_pool(name="psum", bufs=1))

        def sb(name, shape, dtype, tag=None):
            return keep.tile(shape, dtype, name=name, tag=tag or name, align_bytes=64)

        def bank(index, name):
            return psum.tile([P, BANK], F32, name=name, tag="bank%d" % index)

        picks = sb("picks", [P, S // LIST_ROWS], U16)
        donors = sb("donors", [P, PAIRS // LIST_ROWS], U16)
        receivers = sb("receivers", [P, PAIRS // LIST_ROWS], U16)
        table = [sb("table%d" % a, [P, T], I32) for a in range(PASSES)]
        table_scale = sb("table_scale", [P, T], U8)
        w1_raw = [sb("w1_raw%d" % a, [P, PACK, H], F32) for a in range(PASSES - 1)]
        w1_last = [sb("w1_last%d" % u, [P, PACK, H // 2], F32) for u in range(2)]
        w2_raw = sb("w2_raw", [P, 2 * H], U8)
        w2_scale_raw = sb("w2_scale_raw", [P, H], U8)
        gain_sb = sb("gain_sb", [P, PACK], F32)
        amp_sb = sb("amp_sb", [P, PACK], F32)
        wga_sb = sb("wga_sb", [P, PAIRS], F32)
        wgb_sb = sb("wgb_sb", [P, PAIRS], F32)

        nc.vector.memset(table_scale[:].bitcast(I32), 0)
        nc.vector.memset(w2_scale_raw[:].bitcast(I32), 0)

        def load_table(a):
            nc.sync.dma_start(table[a][:], tab_words[a].rearrange("p t j -> p (t j)").bitcast(I32))

        def w1_rows(a):
            return w1[a * P * PACK : (a + 1) * P * PACK, :].rearrange("(p j) c -> p j c", j=PACK)

        load_table(0)
        nc.sync.dma_start(picks[:], offs)
        nc.sync.dma_start(w2_raw[:].bitcast(I32), w2_words[0].bitcast(I32))
        load_table(1)
        nc.sync.dma_start(w1_raw[0][:], w1_rows(0))
        nc.sync.dma_start(w1_raw[1][:], w1_rows(1))
        load_table(2)
        for u in range(2):
            nc.sync.dma_start(w1_last[u][:], w1_rows(PASSES - 1)[:, :, u * (H // 2) : (u + 1) * (H // 2)])
        nc.sync.dma_start(gain_sb[:], gain.rearrange("(p i) -> p i", i=PACK))
        nc.sync.dma_start(receivers[:], offs3)
        nc.sync.dma_start(wgb_sb[:], wgb)
        nc.sync.dma_start(donors[:], offs2)
        nc.sync.dma_start(wga_sb[:], wga)
        nc.sync.dma_start(amp_sb[:], amp.rearrange("(p i) -> p i", i=PACK))

        for quad in range(QUADRANTS):
            rows = slice(SCALE_ROWS * quad, SCALE_ROWS * (quad + 1))
            nc.gpsimd.dma_start(
                table_scale[QUADRANT * quad : QUADRANT * quad + SCALE_ROWS * PASSES, :].bitcast(I32),
                tab_scales[:, rows, :].bitcast(I32),
            )
        for quad in range(QUADRANTS):
            rows = slice(SCALE_ROWS * quad, SCALE_ROWS * (quad + 1))
            nc.gpsimd.dma_start(
                w2_scale_raw[QUADRANT * quad : QUADRANT * quad + SCALE_ROWS, :].bitcast(I32),
                w2_scales[0, rows, :].bitcast(I32),
            )

        identity = sb("identity", [P, P], F32)
        make_identity(nc, identity[:])

        v_scale = sb("v_scale", [P, S], U8)
        nc.vector.tensor_copy(v_scale[:], table_scale[:].indirect(picks[:]))

        w2_codes = sb("w2_codes", [P, 2 * H], U8)
        w2_scale = sb("w2_scale", [P, H], U8)
        nc.vector.tensor_copy(
            w2_codes[:].bitcast(U16).rearrange("p (i q) -> p i q", i=PACK),
            w2_raw[:].bitcast(U16).rearrange("p (q i) -> p i q", i=PACK),
        )
        nc.vector.tensor_copy(
            w2_scale[:].rearrange("p (i q) -> p i q", i=PACK),
            w2_scale_raw[:].rearrange("p (q i) -> p i q", i=PACK),
        )

        v_words = [[sb("v_words%d_%d" % (a, u), [P, BANK], U32) for u in range(HALVES)] for a in range(PASSES)]
        w1_bf = [sb("w1_bf%d" % a, [P, PACK, P, PACK], BF16) for a in range(PASSES)]
        w1_codes = [[sb("w1_codes%d_%d" % (a, i), [P, P], U32) for i in range(PACK)] for a in range(PASSES)]
        w1_scale = [[sb("w1_scale%d_%d" % (a, i), [P, P], U8) for i in range(PACK)] for a in range(PASSES)]
        h_banks = [[bank(HALVES * i + u, "h_bank%d_%d" % (i, u)) for u in range(HALVES)] for i in range(PACK)]

        for a in range(PASSES):
            for u in range(HALVES):
                entries = picks[:, u * BANK // LIST_ROWS : (u + 1) * BANK // LIST_ROWS]
                nc.vector.tensor_copy(v_words[a][u][:], table[a][:].bitcast(U32).indirect(entries))
            dealt = w1_bf[a][:].rearrange("p i q j -> p q i j")
            if a < PASSES - 1:
                loaded = w1_raw[a][:].rearrange("p j (q i) -> p q i j", i=PACK)
                nc.vector.tensor_copy(dealt[:, 0:CAST_SPLIT], loaded[:, 0:CAST_SPLIT])
                nc.scalar.copy(dealt[:, CAST_SPLIT:P], loaded[:, CAST_SPLIT:P])
            else:
                early, late = (piece[:].rearrange("p j (q i) -> p q i j", i=PACK) for piece in w1_last)
                nc.scalar.copy(dealt[:, 0 : P // 2], early)
                nc.vector.tensor_copy(dealt[:, P // 2 : P, 0], late[:, :, 0])
                nc.scalar.copy(dealt[:, P // 2 : P, 1:PACK], late[:, :, 1:PACK])
            for i in range(PACK):
                nc.vector.quantize_mx(
                    out=w1_codes[a][i][:].bitcast(FP8X4),
                    scales=w1_scale[a][i][:],
                    in_=w1_bf[a][:, i].rearrange("p q j -> p (q j)"),
                )
            for i in range(PACK):
                for u in range(HALVES):
                    nc.tensor.matmul_mx(
                        out=h_banks[i][u][:],
                        lhsT=w1_codes[a][i][:].bitcast(FP8X4),
                        lhsT_scale=w1_scale[a][i][:],
                        rhs=v_words[a][u][:].bitcast(FP8X4),
                        rhs_scale=v_scale[SCALE_ROWS * a : P, u * BANK : (u + 1) * BANK],
                        start=(a == 0),
                        stop=(a == PASSES - 1),
                    )

        h = [sb("h%d" % i, [P, S], F32) for i in range(PACK)]
        for i in range(PACK):
            for u in range(HALVES):
                cols = slice(u * BANK, (u + 1) * BANK)
                if (i, u) == (0, HALVES - 1):
                    nc.vector.tensor_scalar(h[i][:, cols], h_banks[i][u][:], gain_sb[:, i : i + 1], None, ALU.mult)
                else:
                    nc.scalar.activation(h[i][:, cols], h_banks[i][u][:], ACT.Copy, scale=gain_sb[:, i : i + 1])

        out_planes = out.rearrange("(p i) m -> p i m", i=PACK)

        def pick(xa, xb, i, chunk):
            start, width = chunk
            entries = slice(start // LIST_ROWS, (start + width) // LIST_ROWS)
            pairs = slice(start, start + width)
            nc.vector.tensor_tensor(xb, h[i][:].indirect(receivers[:, entries]), wgb_sb[:, pairs], ALU.mult)
            nc.vector.tensor_tensor(xa, h[i][:].indirect(donors[:, entries]), wga_sb[:, pairs], ALU.mult)

        def scale_by_amp(x_planes, sines, first):
            for s in range(x_planes.shape[1]):
                i = first + s
                nc.scalar.activation(x_planes[:, s, :], sines[:, s, :], ACT.Copy, scale=amp_sb[:, i : i + 1])

        def activate(xa, xb, total, sines, x_planes, first):
            nc.vector.tensor_tensor(total, xa, xb, ALU.add)
            nc.scalar.activation(sines, total, ACT.Sin)
            scale_by_amp(x_planes, sines, first)

        def activate_turned(name, banks, xa, xb, x_planes, first):
            count, width = xa.shape[1], xa.shape[2]
            blocks = [(s, b) for s in range(count) for b in range(width // P)]
            turned = bank(banks[0], name + "_turned")
            for n, (s, b) in enumerate(blocks):
                for side, closes in ((xb, False), (xa, True)):
                    nc.tensor.matmul(
                        turned[:, n * P : (n + 1) * P],
                        side[:, s, b * P : (b + 1) * P],
                        identity[:],
                        start=not closes,
                        stop=closes,
                        is_transpose=True,
                    )
            turned_sines = sb(name + "_sines", [P, count * width], F32)
            nc.scalar.activation(turned_sines[:], turned[:, 0 : count * width], ACT.Sin)
            back = bank(banks[1], name + "_back")
            for n in range(len(blocks)):
                nc.tensor.transpose(back[:, n * P : (n + 1) * P], turned_sines[:, n * P : (n + 1) * P], identity[:])
            scale_by_amp(x_planes, back[:, 0 : count * width].rearrange("p (s m) -> p s m", s=count), first)

        def interleave(x_bf, x_planes):
            nc.scalar.copy(x_bf[:], x_planes[:].rearrange("p i m -> p m i"))

        def quantize_x(name, x_bf):
            width = x_bf.shape[1]
            x_codes = sb(name + "_codes", [P, width], U32)
            x_scale = sb(name + "_scale", [P, width], U8)
            nc.vector.quantize_mx(
                out=x_codes[:].bitcast(FP8X4), scales=x_scale[:], in_=x_bf[:].rearrange("p m i -> p (m i)")
            )
            return x_codes, x_scale

        def mix(name, bank_index, x_quantized, first, count):
            x_codes, x_scale = x_quantized
            width = x_codes.shape[1]
            y = bank(bank_index, name)
            for s in range(count):
                i = first + s
                nc.tensor.matmul_mx(
                    out=y[:, s * width : (s + 1) * width],
                    lhsT=w2_codes[:, 2 * P * i : 2 * P * (i + 1)].bitcast(FP4X4),
                    lhsT_scale=w2_scale[:, P * i : P * (i + 1)],
                    rhs=x_codes[:].bitcast(FP8X4),
                    rhs_scale=x_scale[:],
                    start=True,
                    stop=True,
                )
            return y[:, 0 : count * width].rearrange("p (i m) -> p i m", i=count)

        def weigh_and_store(name, y, xb, first, chunk, tag=None):
            start, width = chunk
            result = sb(name, list(y.shape), F32, tag)
            nc.vector.tensor_tensor(result[:], y, xb, ALU.mult)
            nc.sync.dma_start(out_planes[:, first : first + y.shape[1], start : start + width], result[:])

        chunk0, chunk1, chunk2 = CHUNKS
        low, high, final = slice(0, 2), slice(2, PACK), slice(LAST, PACK)

        width = chunk0[1]
        xa0 = sb("xa0", [P, LAST, width], F32)
        xa0_last = sb("xa0_last", [P, 1, width], F32, "after_sum0")
        xb0 = sb("xb0", [P, PACK, width], F32)
        total0 = sb("total0", [P, 1, width], F32, "after_sine0")
        sines0 = sb("sines0", [P, 1, width], F32)
        x_planes0 = sb("x_planes0", [P, PACK, width], BF16)
        x_bf0 = sb("x_bf0", [P, width, PACK], BF16, "after_quantize0")
        for i in range(LAST):
            pick(xa0[:, i, :], xb0[:, i, :], i, chunk0)
        pick(xa0_last[:, 0, :], xb0[:, LAST, :], LAST, chunk0)
        activate_turned("low0", (0, 2), xa0[:, low], xb0[:, low], x_planes0[:, low], 0)
        activate_turned("mid0", (1, 3), xa0[:, 2:LAST], xb0[:, 2:LAST], x_planes0[:, 2:LAST], 2)
        activate(xa0_last[:], xb0[:, final], total0[:], sines0[:], x_planes0[:, final], LAST)
        interleave(x_bf0, x_planes0)

        width = chunk1[1]
        sides1 = sb("sides1", [P, 2, PACK, width], F32, "after_sum0")
        xa1, xb1 = sides1[:, 0], sides1[:, 1]
        total1 = sb("total1", [P, 1, width], F32)
        sines1 = sb("sines1", [P, 1, width], F32)
        x_planes1 = sb("x_planes1", [P, PACK, width], BF16)
        x_bf1 = sb("x_bf1", [P, width, PACK], BF16)
        for i in range(PACK):
            pick(xa1[:, i, :], xb1[:, i, :], i, chunk1)
        activate_turned("low1", (4, 5), xa1[:, 0:LAST], xb1[:, 0:LAST], x_planes1[:, 0:LAST], 0)
        activate(xa1[:, final], xb1[:, final], total1[:], sines1[:], x_planes1[:, final], LAST)
        interleave(x_bf1, x_planes1)

        width = chunk2[1]
        total2 = sb("total2", [P, PACK, width], F32)
        sines2 = sb("sines2", [P, PACK, width], F32)
        x_planes2 = sb("x_planes2", [P, PACK, width], BF16)
        x_bf2 = sb("x_bf2", [P, width, PACK], BF16, "after_quantize2")
        sides2_low = sb("sides2_low", [P, 2, 2, width], F32, "after_sine0")
        xa2_low, xb2_low = sides2_low[:, 0], sides2_low[:, 1]
        for i in range(2):
            pick(xa2_low[:, i, :], xb2_low[:, i, :], i, chunk2)
        activate(xa2_low, xb2_low, total2[:, low], sines2[:, low], x_planes2[:, low], 0)

        x0 = quantize_x("x0", x_bf0)
        y0 = [mix("y0_%d" % b, 6 + b, x0, 2 * b, 2) for b in range(2)]

        sides2_high = sb("sides2_high", [P, 3, width], F32, "after_quantize0")
        xa2_last = sb("xa2_last", [P, 1, width], F32, "after_last_sum")
        xb2_high = sides2_high[:, 0:2]
        for i, xa in ((2, sides2_high[:, 2:3]), (LAST, xa2_last[:])):
            plane = slice(i, i + 1)
            xb = xb2_high[:, i - 2 : i - 1]
            pick(xa[:, 0, :], xb[:, 0, :], i, chunk2)
            activate(xa, xb, total2[:, plane], sines2[:, plane], x_planes2[:, plane], i)

        x1 = quantize_x("x1", x_bf1)
        y1 = mix("y1", 0, x1, 0, PACK)
        weigh_and_store("result0_low", y0[0], xb0[:, low], 0, chunk0, "after_last_sum")
        weigh_and_store("result0_high", y0[1], xb0[:, high], 2, chunk0)

        interleave(x_bf2, x_planes2)
        x2 = quantize_x("x2", x_bf2)
        y2 = [mix("y2_%d" % b, 1 + b, x2, 2 * b, 2) for b in range(2)]
        weigh_and_store("result1", y1, xb1, 0, chunk1, "after_quantize2")
        weigh_and_store("result2_low", y2[0], xb2_low, 0, chunk2)
        weigh_and_store("result2_high", y2[1], xb2_high, 2, chunk2)
